import numpy as np
import ml_dtypes


def mxq(x, axis, fmt="e4m3"):
    dtype, down = {"e4m3": (ml_dtypes.float8_e4m3fn, 7), "e5m2": (ml_dtypes.float8_e5m2, 14)}[fmt]
    v = np.moveaxis(np.asarray(x, np.float32).astype(ml_dtypes.bfloat16).astype(np.float64), axis, -1)
    blocks = v.reshape(v.shape[:-1] + (-1, 32))
    amax = np.abs(blocks).max(-1, keepdims=True)
    byte = np.maximum(np.where(amax > 0, np.frexp(amax)[1] - 1 + 127, 0) - down, 1)
    scale = np.exp2(byte - 127.0)
    codes = (blocks / scale).astype(np.float32).astype(dtype).astype(np.float64)
    return np.moveaxis((codes * scale).reshape(v.shape), -1, axis)


WIDE = False


def mx_kscale(k):
    if not WIDE:
        return np.ones(k)
    levels = np.array([10, -10, 5, -5, 0])
    if k % 512:
        return np.exp2(np.random.permutation(np.resize(levels, k // 32))).repeat(32)
    a = np.empty((k // 512, 16))
    for p in range(k // 512):
        a[p, :8] = np.random.permutation(np.resize(levels, 8))
        for g in range(8):
            far = levels[np.abs(levels - a[p, g]) >= 10]
            a[p, g + 8] = far[np.random.randint(len(far))]
    return np.exp2(a.ravel()).repeat(32)


def f64(x):
    return np.asarray(x).astype(np.float64)


def striped8(idx):
    return np.concatenate([v.reshape(-1, 16).T for v in idx]).astype(np.uint16)


def unstriped8(offs):
    return np.stack([offs[16 * g:16 * g + 16].T.reshape(-1) for g in range(8)]).astype(np.int64)


K, M, T, S = 2048, 1024, 1024, 512


def setup_inputs():
    n = np.random.standard_normal
    s = mx_kscale(K)[:, None]
    return {
        "x": (n((K, S)) * s).astype(np.float32),
        "w": (n((K, M)) / np.sqrt(K) / s).astype(np.float32),
        "b": (0.3 * n(1024)).astype(np.float32),
        "wgo": np.repeat(np.random.uniform(0.5, 2.0, (8, S)), 16, axis=0).astype(np.float32),
        "offs": striped8(np.stack([np.random.permutation(T)[:S] for _ in range(8)])),
    }


def reference(x, w, b, wgo, offs):
    x_ = mxq(f64(x), 0, "e4m3")
    w_ = mxq(f64(w), 0, "e4m3")
    y = w_.T @ x_
    place = unstriped8(offs)[np.arange(M) % 128 // 16]
    out = np.zeros((M, T))
    out[np.arange(M)[:, None], place] = f64(wgo)[np.arange(M) % 128] * (y + f64(b)[:, None])
    return out

@@ -1,0 +1,169 @@
+from contextlib import ExitStack
+
+import concourse.mybir as mybir
+from concourse.masks import make_identity
+
+K, M, T, S = 2048, 1024, 1024, 512
+FLOPS = 2 * K * M * S
+
+F32 = mybir.dt.float32
+BF16 = mybir.dt.bfloat16
+U32 = mybir.dt.uint32
+U16 = mybir.dt.uint16
+U8 = mybir.dt.uint8
+FP8X4 = mybir.dt.float8_e4m3fn_x4
+IDENTITY = mybir.ActivationFunctionType.Identity
+MULT = mybir.AluOpType.mult
+
+P = 128
+PACK = 4
+K_PASS = P * PACK
+PASSES = K // K_PASS
+BLOCKS = M // P
+HALF = S // 2
+CHUNKS = [[0], [1], [2], [3], [4, 5], [6, 7]]
+WINDOWS = 6
+
+
+def interleave(copy, grouped, raw):
+    copy(
+        out=grouped.rearrange("p (c i j) -> p c j i", i=4, j=PACK),
+        in_=raw.rearrange("p j (c i) -> p c j i", i=4),
+    )
+
+
+def tile_list_hscat_bias_kernel(tc, x, w, b, wgo, offs, out):
+    nc = tc.nc
+    with ExitStack() as ctx:
+        keep = ctx.enter_context(tc.tile_pool(name="keep", bufs=1))
+        psum = ctx.enter_context(tc.psum_pool(name="psum", bufs=4))
+        psum_b = ctx.enter_context(tc.psum_pool(name="psum_b", bufs=1))
+
+        offsets = keep.tile([P, S // 16], U16, name="offsets")
+        weights = keep.tile([P, S], F32, name="weights")
+        b_rows = keep.tile([P, P], F32, name="b_rows")
+        ident = keep.tile([P, P], F32, name="ident")
+        b_cols = keep.tile([P, BLOCKS], F32, name="b_cols")
+        windows = [keep.tile([P, T], F32, name=f"window{i}") for i in range(WINDOWS)]
+        x_raw = [keep.tile([P, PACK, S], F32, name=f"x_raw{a}") for a in range(PASSES)]
+        w_raw = {}
+        for q, chunk in enumerate(CHUNKS):
+            for a in range(PASSES):
+                w_raw[q, a] = keep.tile([P, PACK, P * len(chunk)], F32, name=f"w_raw{q}_{a}")
+
+        def load_x(a):
+            nc.sync.dma_start(
+                out=x_raw[a][:], in_=x[a * K_PASS : (a + 1) * K_PASS, :].rearrange("(p j) c -> p j c", j=PACK)
+            )
+
+        def load_w(q, a):
+            c0 = CHUNKS[q][0] * P
+            c1 = c0 + P * len(CHUNKS[q])
+            nc.sync.dma_start(
+                out=w_raw[q, a][:],
+                in_=w[a * K_PASS : (a + 1) * K_PASS, c0:c1].rearrange("(p j) c -> p j c", j=PACK),
+            )
+
+        nc.gpsimd.memset(b_rows[:], 0.0)
+        make_identity(nc, ident[:])
+
+        for a in range(PASSES - 1):
+            load_w(0, a)
+            load_x(a)
+        load_x(PASSES - 1)
+        load_w(0, PASSES - 1)
+        nc.sync.dma_start(offsets[:], offs)
+        nc.sync.dma_start(out=b_rows[0:BLOCKS, :], in_=b.rearrange("(c p) -> c p", p=P))
+        nc.sync.dma_start(out=weights[:], in_=wgo)
+        for q in range(1, len(CHUNKS)):
+            for a in range(PASSES):
+                load_w(q, a)
+
+        for i in range(WINDOWS):
+            (nc.vector if i < 4 else nc.gpsimd).memset(windows[i][:], 0.0)
+
+        bt = psum_b.tile([P, P], F32, name="bt")
+        nc.tensor.transpose(bt[:], b_rows[:], ident[:])
+        nc.scalar.copy(out=b_cols[:], in_=bt[:, 0:BLOCKS])
+
+        x_codes = keep.tile([P, PASSES, S], U32, align_bytes=64, name="x_codes")
+        x_scales = keep.tile([P, PASSES, S], U8, align_bytes=64, name="x_scales")
+        w_codes, w_scales, w_grouped = {}, {}, {}
+        for q, chunk in enumerate(CHUNKS):
+            width = P * len(chunk)
+            w_codes[q] = keep.tile([P, PASSES, width], U32, align_bytes=64, name=f"w_codes{q}")
+            w_scales[q] = keep.tile([P, PASSES, width], U8, align_bytes=64, name=f"w_scales{q}")
+            w_grouped[q] = keep.tile([P, PASSES, width * PACK], BF16, align_bytes=64, name=f"w_grouped{q}")
+
+        def prep_x(a):
+            for h, copy in ((0, nc.vector.tensor_copy), (1, nc.scalar.copy)):
+                cols = slice(h * HALF, (h + 1) * HALF)
+                grouped = keep.tile([P, HALF * PACK], BF16, align_bytes=64, name=f"x_grouped{a}_{h}")
+                interleave(copy, grouped[:], x_raw[a][:, :, cols])
+                nc.vector.quantize_mx(
+                    out=x_codes[:, a, cols].bitcast(FP8X4), scales=x_scales[:, a, cols], in_=grouped[:]
+                )
+
+        def group_w(q, a, copy):
+            interleave(copy, w_grouped[q][:, a, :], w_raw[q, a][:])
+
+        def quantize_w(q, a0, a1):
+            nc.vector.quantize_mx(
+                out=w_codes[q][:, a0:a1, :].rearrange("p a c -> p (a c)").bitcast(FP8X4),
+                scales=w_scales[q][:, a0:a1, :].rearrange("p a c -> p (a c)"),
+                in_=w_grouped[q][:, a0:a1, :].rearrange("p a c -> p (a c)"),
+            )
+
+        def product(q, i):
+            blk = CHUNKS[q][i]
+            cols = slice(i * P, (i + 1) * P)
+            acc = psum.tile([P, S], F32, name="acc")
+            for a in range(PASSES):
+                nc.tensor.matmul_mx(
+                    out=acc[:],
+                    lhsT=w_codes[q][:, a, cols].bitcast(FP8X4),
+                    lhsT_scale=w_scales[q][:, a, cols],
+                    rhs=x_codes[:, a, :].bitcast(FP8X4),
+                    rhs_scale=x_scales[:, a, :],
+                    start=(a == 0),
+                    stop=(a == PASSES - 1),
+                )
+            y = keep.tile([P, S], F32, name=f"y{blk}")
+            for c0, c1 in ((0, HALF), (HALF, S)) if blk == 0 else ((0, S),):
+                nc.scalar.activation(out=y[:, c0:c1], in_=acc[:, c0:c1], func=IDENTITY, bias=b_cols[:, blk : blk + 1])
+            return y
+
+        def place(blk, y):
+            window = windows[blk % WINDOWS]
+            for h in range(2):
+                cols = slice(h * HALF, (h + 1) * HALF)
+                nc.vector.tensor_tensor(
+                    window[:].indirect(offsets[:, h * HALF // 16 : (h + 1) * HALF // 16]),
+                    y[:, cols],
+                    weights[:, cols],
+                    MULT,
+                )
+            nc.sync.dma_start(out=out[blk * P : (blk + 1) * P, :], in_=window[:])
+
+        for a in range(PASSES):
+            if a < PASSES - 1:
+                group_w(0, a, nc.scalar.copy)
+                quantize_w(0, a, a + 1)
+                prep_x(a)
+            else:
+                prep_x(a)
+                group_w(0, a, nc.vector.tensor_copy)
+                quantize_w(0, a, a + 1)
+        pending = [(0, product(0, 0))]
+        for q in range(1, len(CHUNKS)):
+            for a in range(PASSES):
+                group_w(q, a, nc.scalar.copy)
+            step = PASSES // len(CHUNKS[q])
+            for a0 in range(0, PASSES, step):
+                quantize_w(q, a0, a0 + step)
+            ready = [(CHUNKS[q][i], product(q, i)) for i in range(len(CHUNKS[q]))]
+            for blk, y in pending:
+                place(blk, y)
+            pending = ready
+        for blk, y in pending:
+            place(blk, y)

@@ -21,7 +21,6 @@ K_PASS = P * PACK
 PASSES = K // K_PASS
 BLOCKS = M // P
 HALF = S // 2
-CHUNKS = [[0], [1], [2], [3], [4, 5], [6, 7]]
 WINDOWS = 6
 
 
@@ -46,66 +45,40 @@ def tile_list_hscat_bias_kernel(tc, x, w, b, wgo, offs, out):
         b_cols = keep.tile([P, BLOCKS], F32, name="b_cols")
         windows = [keep.tile([P, T], F32, name=f"window{i}") for i in range(WINDOWS)]
         x_raw = [keep.tile([P, PACK, S], F32, name=f"x_raw{a}") for a in range(PASSES)]
-        w_raw = {}
-        for q, chunk in enumerate(CHUNKS):
-            for a in range(PASSES):
-                w_raw[q, a] = keep.tile([P, PACK, P * len(chunk)], F32, name=f"w_raw{q}_{a}")
-
-        def load_x(a):
-            nc.sync.dma_start(
-                out=x_raw[a][:], in_=x[a * K_PASS : (a + 1) * K_PASS, :].rearrange("(p j) c -> p j c", j=PACK)
-            )
-
-        def load_w(q, a):
-            c0 = CHUNKS[q][0] * P
-            c1 = c0 + P * len(CHUNKS[q])
-            nc.sync.dma_start(
-                out=w_raw[q, a][:],
-                in_=w[a * K_PASS : (a + 1) * K_PASS, c0:c1].rearrange("(p j) c -> p j c", j=PACK),
-            )
-
-        nc.gpsimd.memset(b_rows[:], 0.0)
-        make_identity(nc, ident[:])
-
-        for a in range(PASSES - 1):
-            load_w(0, a)
-            load_x(a)
-        load_x(PASSES - 1)
-        load_w(0, PASSES - 1)
-        nc.sync.dma_start(offsets[:], offs)
-        nc.sync.dma_start(out=b_rows[0:BLOCKS, :], in_=b.rearrange("(c p) -> c p", p=P))
-        nc.sync.dma_start(out=weights[:], in_=wgo)
-        for q in range(1, len(CHUNKS)):
-            for a in range(PASSES):
-                load_w(q, a)
-
-        for i in range(WINDOWS):
-            (nc.vector if i < 4 else nc.gpsimd).memset(windows[i][:], 0.0)
-
-        bt = psum_b.tile([P, P], F32, name="bt")
-        nc.tensor.transpose(bt[:], b_rows[:], ident[:])
-        nc.scalar.copy(out=b_cols[:], in_=bt[:, 0:BLOCKS])
-
+        w_raw = [[keep.tile([P, PACK, P], F32, name=f"w_raw{q}_{a}") for a in range(PASSES)] for q in range(BLOCKS)]
         x_codes = keep.tile([P, PASSES, S], U32, align_bytes=64, name="x_codes")
         x_scales = keep.tile([P, PASSES, S], U8, align_bytes=64, name="x_scales")
-        w_codes, w_scales, w_grouped = {}, {}, {}
-        for q, chunk in enumerate(CHUNKS):
-            width = P * len(chunk)
-            w_codes[q] = keep.tile([P, PASSES, width], U32, align_bytes=64, name=f"w_codes{q}")
-            w_scales[q] = keep.tile([P, PASSES, width], U8, align_bytes=64, name=f"w_scales{q}")
-            w_grouped[q] = keep.tile([P, PASSES, width * PACK], BF16, align_bytes=64, name=f"w_grouped{q}")
+        x_grouped = [keep.tile([P, S * PACK], BF16, align_bytes=64, name=f"x_grouped{a}") for a in range(PASSES)]
+        w_codes = [keep.tile([P, PASSES, P], U32, align_bytes=64, name=f"w_codes{q}") for q in range(BLOCKS)]
+        w_scales = [keep.tile([P, PASSES, P], U8, align_bytes=64, name=f"w_scales{q}") for q in range(BLOCKS)]
+        w_grouped = [keep.tile([P, PASSES, P * PACK], BF16, align_bytes=64, name=f"w_grouped{q}") for q in range(BLOCKS)]
+        y = [keep.tile([P, S], F32, name=f"y{q}") for q in range(BLOCKS)]
 
-        def prep_x(a):
-            for h, copy in ((0, nc.vector.tensor_copy), (1, nc.scalar.copy)):
-                cols = slice(h * HALF, (h + 1) * HALF)
-                grouped = keep.tile([P, HALF * PACK], BF16, align_bytes=64, name=f"x_grouped{a}_{h}")
-                interleave(copy, grouped[:], x_raw[a][:, :, cols])
-                nc.vector.quantize_mx(
-                    out=x_codes[:, a, cols].bitcast(FP8X4), scales=x_scales[:, a, cols], in_=grouped[:]
-                )
+        def load_x(a):
+            rows = x[a * K_PASS : (a + 1) * K_PASS, :]
+            nc.sync.dma_start(out=x_raw[a][:], in_=rows.rearrange("(p j) c -> p j c", j=PACK))
+
+        def load_w(q, a):
+            rows = w[a * K_PASS : (a + 1) * K_PASS, q * P : (q + 1) * P]
+            nc.sync.dma_start(out=w_raw[q][a][:], in_=rows.rearrange("(p j) c -> p j c", j=PACK))
+
+        def group_x(a, h, copy):
+            interleave(
+                copy,
+                x_grouped[a][:, h * HALF * PACK : (h + 1) * HALF * PACK],
+                x_raw[a][:, :, h * HALF : (h + 1) * HALF],
+            )
+
+        def quantize_x(a, h):
+            cols = slice(h * HALF, (h + 1) * HALF)
+            nc.vector.quantize_mx(
+                out=x_codes[:, a, cols].bitcast(FP8X4),
+                scales=x_scales[:, a, cols],
+                in_=x_grouped[a][:, h * HALF * PACK : (h + 1) * HALF * PACK],
+            )
 
         def group_w(q, a, copy):
-            interleave(copy, w_grouped[q][:, a, :], w_raw[q, a][:])
+            interleave(copy, w_grouped[q][:, a, :], w_raw[q][a][:])
 
         def quantize_w(q, a0, a1):
             nc.vector.quantize_mx(
@@ -114,56 +87,82 @@ def tile_list_hscat_bias_kernel(tc, x, w, b, wgo, offs, out):
                 in_=w_grouped[q][:, a0:a1, :].rearrange("p a c -> p (a c)"),
             )
 
-        def product(q, i):
-            blk = CHUNKS[q][i]
-            cols = slice(i * P, (i + 1) * P)
-            acc = psum.tile([P, S], F32, name="acc")
-            for a in range(PASSES):
+        def multiply(q, a0, a1, acc):
+            for a in range(a0, a1):
                 nc.tensor.matmul_mx(
                     out=acc[:],
-                    lhsT=w_codes[q][:, a, cols].bitcast(FP8X4),
-                    lhsT_scale=w_scales[q][:, a, cols],
+                    lhsT=w_codes[q][:, a, :].bitcast(FP8X4),
+                    lhsT_scale=w_scales[q][:, a, :],
                     rhs=x_codes[:, a, :].bitcast(FP8X4),
                     rhs_scale=x_scales[:, a, :],
                     start=(a == 0),
                     stop=(a == PASSES - 1),
                 )
-            y = keep.tile([P, S], F32, name=f"y{blk}")
-            for c0, c1 in ((0, HALF), (HALF, S)) if blk == 0 else ((0, S),):
-                nc.scalar.activation(out=y[:, c0:c1], in_=acc[:, c0:c1], func=IDENTITY, bias=b_cols[:, blk : blk + 1])
-            return y
 
-        def place(blk, y):
-            window = windows[blk % WINDOWS]
-            for h in range(2):
-                cols = slice(h * HALF, (h + 1) * HALF)
-                nc.vector.tensor_tensor(
-                    window[:].indirect(offsets[:, h * HALF // 16 : (h + 1) * HALF // 16]),
-                    y[:, cols],
-                    weights[:, cols],
-                    MULT,
-                )
-            nc.sync.dma_start(out=out[blk * P : (blk + 1) * P, :], in_=window[:])
+        def add_bias(q, h, acc):
+            cols = slice(h * HALF, (h + 1) * HALF)
+            nc.scalar.activation(out=y[q][:, cols], in_=acc[:, cols], func=IDENTITY, bias=b_cols[:, q : q + 1])
 
+        def place(q, h):
+            cols = slice(h * HALF, (h + 1) * HALF)
+            nc.vector.tensor_tensor(
+                windows[q % WINDOWS][:].indirect(offsets[:, h * HALF // 16 : (h + 1) * HALF // 16]),
+                y[q][:, cols],
+                weights[:, cols],
+                MULT,
+            )
+
+        def store(q):
+            nc.sync.dma_start(out=out[q * P : (q + 1) * P, :], in_=windows[q % WINDOWS][:])
+
+        nc.gpsimd.memset(b_rows[:], 0.0)
+        make_identity(nc, ident[:])
+        nc.sync.dma_start(out=b_rows[0:BLOCKS, :], in_=b.rearrange("(c p) -> c p", p=P))
+        nc.sync.dma_start(offsets[:], offs)
+        for a in range(PASSES - 1):
+            load_w(0, a)
+            load_x(a)
+        load_x(PASSES - 1)
+        load_w(0, PASSES - 1)
+        nc.sync.dma_start(out=weights[:], in_=wgo)
+        for q in range(1, BLOCKS):
+            for a in range(PASSES):
+                load_w(q, a)
+        for i in range(WINDOWS):
+            (nc.vector if i < 4 else nc.gpsimd).memset(windows[i][:], 0.0)
+
+        vcopy, scopy = nc.vector.tensor_copy, nc.scalar.copy
+        acc = psum.tile([P, S], F32, name="acc")
         for a in range(PASSES):
             if a < PASSES - 1:
-                group_w(0, a, nc.scalar.copy)
+                group_w(0, a, scopy)
+            group_x(a, 1, scopy)
+            group_x(a, 0, vcopy)
+            if a == PASSES - 1:
+                quantize_x(a, 0)
+                group_w(0, a, vcopy)
+                quantize_x(a, 1)
                 quantize_w(0, a, a + 1)
-                prep_x(a)
             else:
-                prep_x(a)
-                group_w(0, a, nc.vector.tensor_copy)
                 quantize_w(0, a, a + 1)
-        pending = [(0, product(0, 0))]
-        for q in range(1, len(CHUNKS)):
-            for a in range(PASSES):
-                group_w(q, a, nc.scalar.copy)
-            step = PASSES // len(CHUNKS[q])
-            for a0 in range(0, PASSES, step):
-                quantize_w(q, a0, a0 + step)
-            ready = [(CHUNKS[q][i], product(q, i)) for i in range(len(CHUNKS[q]))]
-            for blk, y in pending:
-                place(blk, y)
-            pending = ready
-        for blk, y in pending:
-            place(blk, y)
+                quantize_x(a, 0)
+                quantize_x(a, 1)
+            if a == 0:
+                bt = psum_b.tile([P, P], F32, name="bt")
+                nc.tensor.transpose(bt[:], b_rows[:], ident[:])
+                scopy(out=b_cols[:], in_=bt[:, 0:BLOCKS])
+            multiply(0, a, a + 1, acc)
+        for q in range(BLOCKS):
+            last = q + 1 == BLOCKS
+            nxt = None if last else psum.tile([P, S], F32, name="acc")
+            for h in range(2):
+                if not last:
+                    for a in (2 * h, 2 * h + 1):
+                        group_w(q + 1, a, scopy)
+                    quantize_w(q + 1, 2 * h, 2 * h + 2)
+                add_bias(q, h, acc)
+                place(q, h)
+                if not last:
+                    multiply(q + 1, 2 * h, 2 * h + 2, nxt)
+            store(q)
+            acc = nxt

@@ -52,7 +52,6 @@ def tile_list_hscat_bias_kernel(tc, x, w, b, wgo, offs, out):
         w_codes = [keep.tile([P, PASSES, P], U32, align_bytes=64, name=f"w_codes{q}") for q in range(BLOCKS)]
         w_scales = [keep.tile([P, PASSES, P], U8, align_bytes=64, name=f"w_scales{q}") for q in range(BLOCKS)]
         w_grouped = [keep.tile([P, PASSES, P * PACK], BF16, align_bytes=64, name=f"w_grouped{q}") for q in range(BLOCKS)]
-        y = [keep.tile([P, S], F32, name=f"y{q}") for q in range(BLOCKS)]
 
         def load_x(a):
             rows = x[a * K_PASS : (a + 1) * K_PASS, :]
@@ -99,15 +98,15 @@ def tile_list_hscat_bias_kernel(tc, x, w, b, wgo, offs, out):
                     stop=(a == PASSES - 1),
                 )
 
-        def add_bias(q, h, acc):
+        def add_bias(q, h, acc, y):
             cols = slice(h * HALF, (h + 1) * HALF)
-            nc.scalar.activation(out=y[q][:, cols], in_=acc[:, cols], func=IDENTITY, bias=b_cols[:, q : q + 1])
+            nc.scalar.activation(out=y, in_=acc[:, cols], func=IDENTITY, bias=b_cols[:, q : q + 1])
 
-        def place(q, h):
+        def place(q, h, y):
             cols = slice(h * HALF, (h + 1) * HALF)
             nc.vector.tensor_tensor(
                 windows[q % WINDOWS][:].indirect(offsets[:, h * HALF // 16 : (h + 1) * HALF // 16]),
-                y[q][:, cols],
+                y,
                 weights[:, cols],
                 MULT,
             )
@@ -119,11 +118,12 @@ def tile_list_hscat_bias_kernel(tc, x, w, b, wgo, offs, out):
         make_identity(nc, ident[:])
         nc.sync.dma_start(out=b_rows[0:BLOCKS, :], in_=b.rearrange("(c p) -> c p", p=P))
         nc.sync.dma_start(offsets[:], offs)
-        for a in range(PASSES - 1):
-            load_w(0, a)
+        for a in range(PASSES):
             load_x(a)
-        load_x(PASSES - 1)
-        load_w(0, PASSES - 1)
+            if a < 2:
+                load_w(0, a)
+        load_w(0, 2)
+        load_w(0, 3)
         nc.sync.dma_start(out=weights[:], in_=wgo)
         for q in range(1, BLOCKS):
             for a in range(PASSES):
@@ -133,36 +133,46 @@ def tile_list_hscat_bias_kernel(tc, x, w, b, wgo, offs, out):
 
         vcopy, scopy = nc.vector.tensor_copy, nc.scalar.copy
         acc = psum.tile([P, S], F32, name="acc")
+        bt = psum_b.tile([P, P], F32, name="bt")
+        nc.tensor.transpose(bt[:], b_rows[:], ident[:])
         for a in range(PASSES):
-            if a < PASSES - 1:
-                group_w(0, a, scopy)
             group_x(a, 1, scopy)
             group_x(a, 0, vcopy)
-            if a == PASSES - 1:
-                quantize_x(a, 0)
-                group_w(0, a, vcopy)
-                quantize_x(a, 1)
-                quantize_w(0, a, a + 1)
-            else:
-                quantize_w(0, a, a + 1)
-                quantize_x(a, 0)
-                quantize_x(a, 1)
+            if a < 2:
+                group_w(0, a, scopy)
             if a == 0:
-                bt = psum_b.tile([P, P], F32, name="bt")
-                nc.tensor.transpose(bt[:], b_rows[:], ident[:])
                 scopy(out=b_cols[:], in_=bt[:, 0:BLOCKS])
-            multiply(0, a, a + 1, acc)
-        for q in range(BLOCKS):
-            last = q + 1 == BLOCKS
-            nxt = None if last else psum.tile([P, S], F32, name="acc")
-            for h in range(2):
-                if not last:
-                    for a in (2 * h, 2 * h + 1):
-                        group_w(q + 1, a, scopy)
-                    quantize_w(q + 1, 2 * h, 2 * h + 2)
-                add_bias(q, h, acc)
-                place(q, h)
-                if not last:
-                    multiply(q + 1, 2 * h, 2 * h + 2, nxt)
-            store(q)
-            acc = nxt
+            quantize_x(a, 0)
+            quantize_x(a, 1)
+            if a < 2:
+                quantize_w(0, a, a + 1)
+                multiply(0, a, a + 1, acc)
+        group_w(0, 2, scopy)
+        group_w(0, 3, vcopy)
+        quantize_w(0, 2, 3)
+        quantize_w(0, 3, 4)
+        multiply(0, 2, 4, acc)
+        passes = [(1 + i // PASSES, i % PASSES) for i in range((BLOCKS - 1) * PASSES)]
+        accs = [acc]
+        for u in range(2 * BLOCKS):
+            q, h = divmod(u, 2)
+            n = {0: 0, 1: PASSES}.get(u, PASSES // 2)
+            ahead, passes = passes[:n], passes[n:]
+            for nq, a in ahead:
+                group_w(nq, a, scopy)
+                if a % 2 == 1:
+                    quantize_w(nq, a - 1, a + 1)
+            if ahead:
+                nq, a = ahead[-1]
+                y = w_raw[nq][a][:, 0:2, :].rearrange("p j c -> p (j c)")
+            else:
+                own = keep.tile([P, HALF], F32, name=f"y{u}")
+                y = own[:]
+            add_bias(q, h, accs[q], y)
+            place(q, h, y)
+            for nq, a in ahead:
+                if a == 0:
+                    accs.append(psum.tile([P, S], F32, name="acc"))
+                multiply(nq, a, a + 1, accs[nq])
+            if h == 1:
+                store(q)

from contextlib import ExitStack

import concourse.mybir as mybir
from concourse.masks import make_identity

K, M, T, S = 2048, 1024, 1024, 512
FLOPS = 2 * K * M * S

F32 = mybir.dt.float32
BF16 = mybir.dt.bfloat16
U32 = mybir.dt.uint32
U16 = mybir.dt.uint16
U8 = mybir.dt.uint8
FP8X4 = mybir.dt.float8_e4m3fn_x4
IDENTITY = mybir.ActivationFunctionType.Identity
MULT = mybir.AluOpType.mult

P = 128
PACK = 4
K_PASS = P * PACK
PASSES = K // K_PASS
BLOCKS = M // P
HALF = S // 2
WINDOWS = 6


def interleave(copy, grouped, raw):
    copy(
        out=grouped.rearrange("p (c i j) -> p c j i", i=4, j=PACK),
        in_=raw.rearrange("p j (c i) -> p c j i", i=4),
    )


def tile_list_hscat_bias_kernel(tc, x, w, b, wgo, offs, out):
    nc = tc.nc
    with ExitStack() as ctx:
        keep = ctx.enter_context(tc.tile_pool(name="keep", bufs=1))
        psum = ctx.enter_context(tc.psum_pool(name="psum", bufs=4))
        psum_b = ctx.enter_context(tc.psum_pool(name="psum_b", bufs=1))

        offsets = keep.tile([P, S // 16], U16, name="offsets")
        weights = keep.tile([P, S], F32, name="weights")
        b_rows = keep.tile([P, P], F32, name="b_rows")
        ident = keep.tile([P, P], F32, name="ident")
        b_cols = keep.tile([P, BLOCKS], F32, name="b_cols")
        windows = [keep.tile([P, T], F32, name=f"window{i}") for i in range(WINDOWS)]
        x_raw = [keep.tile([P, PACK, S], F32, name=f"x_raw{a}") for a in range(PASSES)]
        w_raw = [[keep.tile([P, PACK, P], F32, name=f"w_raw{q}_{a}") for a in range(PASSES)] for q in range(BLOCKS)]
        x_codes = keep.tile([P, PASSES, S], U32, align_bytes=64, name="x_codes")
        x_scales = keep.tile([P, PASSES, S], U8, align_bytes=64, name="x_scales")
        x_grouped = [keep.tile([P, S * PACK], BF16, align_bytes=64, name=f"x_grouped{a}") for a in range(PASSES)]
        w_codes = [keep.tile([P, PASSES, P], U32, align_bytes=64, name=f"w_codes{q}") for q in range(BLOCKS)]
        w_scales = [keep.tile([P, PASSES, P], U8, align_bytes=64, name=f"w_scales{q}") for q in range(BLOCKS)]
        w_grouped = [keep.tile([P, PASSES, P * PACK], BF16, align_bytes=64, name=f"w_grouped{q}") for q in range(BLOCKS)]

        def load_x(a):
            rows = x[a * K_PASS : (a + 1) * K_PASS, :]
            nc.sync.dma_start(out=x_raw[a][:], in_=rows.rearrange("(p j) c -> p j c", j=PACK))

        def load_w(q, a):
            rows = w[a * K_PASS : (a + 1) * K_PASS, q * P : (q + 1) * P]
            nc.sync.dma_start(out=w_raw[q][a][:], in_=rows.rearrange("(p j) c -> p j c", j=PACK))

        def group_x(a, h, copy):
            interleave(
                copy,
                x_grouped[a][:, h * HALF * PACK : (h + 1) * HALF * PACK],
                x_raw[a][:, :, h * HALF : (h + 1) * HALF],
            )

        def quantize_x(a, h):
            cols = slice(h * HALF, (h + 1) * HALF)
            nc.vector.quantize_mx(
                out=x_codes[:, a, cols].bitcast(FP8X4),
                scales=x_scales[:, a, cols],
                in_=x_grouped[a][:, h * HALF * PACK : (h + 1) * HALF * PACK],
            )

        def group_w(q, a, copy):
            interleave(copy, w_grouped[q][:, a, :], w_raw[q][a][:])

        def quantize_w(q, a0, a1):
            nc.vector.quantize_mx(
                out=w_codes[q][:, a0:a1, :].rearrange("p a c -> p (a c)").bitcast(FP8X4),
                scales=w_scales[q][:, a0:a1, :].rearrange("p a c -> p (a c)"),
                in_=w_grouped[q][:, a0:a1, :].rearrange("p a c -> p (a c)"),
            )

        def multiply(q, a0, a1, acc):
            for a in range(a0, a1):
                nc.tensor.matmul_mx(
                    out=acc[:],
                    lhsT=w_codes[q][:, a, :].bitcast(FP8X4),
                    lhsT_scale=w_scales[q][:, a, :],
                    rhs=x_codes[:, a, :].bitcast(FP8X4),
                    rhs_scale=x_scales[:, a, :],
                    start=(a == 0),
                    stop=(a == PASSES - 1),
                )

        def add_bias(q, h, acc, y):
            cols = slice(h * HALF, (h + 1) * HALF)
            nc.scalar.activation(out=y, in_=acc[:, cols], func=IDENTITY, bias=b_cols[:, q : q + 1])

        def place(q, h, y):
            cols = slice(h * HALF, (h + 1) * HALF)
            nc.vector.tensor_tensor(
                windows[q % WINDOWS][:].indirect(offsets[:, h * HALF // 16 : (h + 1) * HALF // 16]),
                y,
                weights[:, cols],
                MULT,
            )

        def store(q):
            nc.sync.dma_start(out=out[q * P : (q + 1) * P, :], in_=windows[q % WINDOWS][:])

        nc.gpsimd.memset(b_rows[:], 0.0)
        make_identity(nc, ident[:])
        nc.sync.dma_start(out=b_rows[0:BLOCKS, :], in_=b.rearrange("(c p) -> c p", p=P))
        nc.sync.dma_start(offsets[:], offs)
        for a in range(PASSES):
            load_x(a)
            if a < 2:
                load_w(0, a)
        load_w(0, 2)
        load_w(0, 3)
        nc.sync.dma_start(out=weights[:], in_=wgo)
        for q in range(1, BLOCKS):
            for a in range(PASSES):
                load_w(q, a)
        for i in range(WINDOWS):
            (nc.vector if i < 4 else nc.gpsimd).memset(windows[i][:], 0.0)

        vcopy, scopy = nc.vector.tensor_copy, nc.scalar.copy
        acc = psum.tile([P, S], F32, name="acc")
        bt = psum_b.tile([P, P], F32, name="bt")
        nc.tensor.transpose(bt[:], b_rows[:], ident[:])
        for a in range(PASSES):
            group_x(a, 1, scopy)
            group_x(a, 0, vcopy)
            if a < 2:
                group_w(0, a, scopy)
            if a == 0:
                scopy(out=b_cols[:], in_=bt[:, 0:BLOCKS])
            quantize_x(a, 0)
            quantize_x(a, 1)
            if a < 2:
                quantize_w(0, a, a + 1)
                multiply(0, a, a + 1, acc)
        group_w(0, 2, scopy)
        group_w(0, 3, vcopy)
        quantize_w(0, 2, 3)
        quantize_w(0, 3, 4)
        multiply(0, 2, 4, acc)
        passes = [(1 + i // PASSES, i % PASSES) for i in range((BLOCKS - 1) * PASSES)]
        accs = [acc]
        for u in range(2 * BLOCKS):
            q, h = divmod(u, 2)
            n = {0: 0, 1: PASSES}.get(u, PASSES // 2)
            ahead, passes = passes[:n], passes[n:]
            for nq, a in ahead:
                group_w(nq, a, scopy)
                if a % 2 == 1:
                    quantize_w(nq, a - 1, a + 1)
            if ahead:
                nq, a = ahead[-1]
                y = w_raw[nq][a][:, 0:2, :].rearrange("p j c -> p (j c)")
            else:
                own = keep.tile([P, HALF], F32, name=f"y{u}")
                y = own[:]
            add_bias(q, h, accs[q], y)
            place(q, h, y)
            for nq, a in ahead:
                if a == 0:
                    accs.append(psum.tile([P, S], F32, name="acc"))
                multiply(nq, a, a + 1, accs[nq])
            if h == 1:
                store(q)
